import numpy as np
import ml_dtypes


def mxq(x, axis, fmt="e4m3"):
    dtype, down = {"e4m3": (ml_dtypes.float8_e4m3fn, 7), "e5m2": (ml_dtypes.float8_e5m2, 14)}[fmt]
    v = np.moveaxis(np.asarray(x, np.float32).astype(ml_dtypes.bfloat16).astype(np.float64), axis, -1)
    blocks = v.reshape(v.shape[:-1] + (-1, 32))
    amax = np.abs(blocks).max(-1, keepdims=True)
    byte = np.maximum(np.where(amax > 0, np.frexp(amax)[1] - 1 + 127, 0) - down, 1)
    scale = np.exp2(byte - 127.0)
    codes = (blocks / scale).astype(np.float32).astype(dtype).astype(np.float64)
    return np.moveaxis((codes * scale).reshape(v.shape), -1, axis)


WIDE = False


def mx_kscale(k):
    if not WIDE:
        return np.ones(k)
    levels = np.array([10, -10, 5, -5, 0])
    if k % 512:
        return np.exp2(np.random.permutation(np.resize(levels, k // 32))).repeat(32)
    a = np.empty((k // 512, 16))
    for p in range(k // 512):
        a[p, :8] = np.random.permutation(np.resize(levels, 8))
        for g in range(8):
            far = levels[np.abs(levels - a[p, g]) >= 10]
            a[p, g + 8] = far[np.random.randint(len(far))]
    return np.exp2(a.ravel()).repeat(32)


def f64(x):
    return np.asarray(x).astype(np.float64)


def striped(idx):
    return np.tile(idx.reshape(-1, 16).T, (8, 1)).astype(np.uint16)


def unstriped(offs):
    return offs[:16].T.reshape(-1).astype(np.int64)


E2M1 = np.array([0.0, 0.5, 1.0, 1.5, 2.0, 3.0, 4.0, 6.0, -0.0, -0.5, -1.0, -1.5, -2.0, -3.0, -4.0, -6.0])


def pack_weight(w, fmt):
    k, n = w.shape
    w = f64(np.asarray(w, np.float32).astype(ml_dtypes.bfloat16)).reshape(k // 32, 32, n)
    amax = np.abs(w).max(1)
    if fmt == "e4m3":
        byte = np.frexp(amax)[1] - 1 + 127 - 7
    else:
        mant, ex = np.frexp(amax / 6.0)
        byte = np.where(mant > 0.5, ex, ex - 1) + 127
    byte = np.clip(np.where(amax > 0, byte, 1), 1, 254)
    scaled = (w * np.exp2(127.0 - byte)[:, None, :]).reshape(k, n).astype(np.float32)
    by_word = np.ascontiguousarray(scaled.reshape(k // 512, 128, 4, n).transpose(0, 1, 3, 2))
    if fmt == "e4m3":
        words = by_word.astype(ml_dtypes.float8_e4m3fn).view(np.uint8)
    else:
        c = by_word.astype(ml_dtypes.float4_e2m1fn).view(np.uint8) & 0xF
        words = (c[..., 0::2] | (c[..., 1::2] << 4)).reshape(k // 512, 128, 2 * n)
    return np.ascontiguousarray(words), np.ascontiguousarray(byte.astype(np.uint8).reshape(k // 512, 16, n))


def unpack_weight(words, scales, fmt):
    g, _, n = scales.shape
    words = np.ascontiguousarray(words).reshape(g, 128, n, -1)
    if fmt == "e4m3":
        vals = words.view(ml_dtypes.float8_e4m3fn).astype(np.float64)
    else:
        nib = np.empty((g, 128, n, 4), np.uint8)
        nib[..., 0::2] = words & 0xF
        nib[..., 1::2] = words >> 4
        vals = E2M1[nib]
    vals = vals * np.repeat(np.exp2(scales.astype(np.float64) - 127.0), 8, axis=1)[..., None]
    return vals.transpose(0, 1, 3, 2).reshape(g * 512, n)


def gelu(v):
    return 0.5 * v * (1.0 + np.tanh(np.sqrt(2.0 / np.pi) * (v + 0.044715 * v**3)))


K, T, S, H, N = 1024, 4096, 1024, 1024, 512

def setup_inputs():
    n = np.random.standard_normal
    s = mx_kscale(K)[:, None]
    u = mx_kscale(H)[:, None]
    tab_words, tab_scales = pack_weight(n((K, T)) * s, "e2m1")
    w2_words, w2_scales = pack_weight(n((K, H)) / np.sqrt(K) / s, "e4m3")
    w3_words, w3_scales = pack_weight(1.5 * n((H, N)) / np.sqrt(H) / u, "e2m1")
    return {
        "tab_words": tab_words, "tab_scales": tab_scales,
        "offs": striped(np.random.permutation(T)[:S]),
        "offs2": striped(np.random.permutation(T)[:S]),
        "w1": (0.5 * n((K, H)) / np.sqrt(K) / s).astype(np.float32),
        "w2_words": w2_words, "w2_scales": w2_scales,
        "gain": (np.exp(0.3 * n(H)) * u[:, 0]).astype(np.float32),
        "w3_words": w3_words, "w3_scales": w3_scales,
        "back": (0.7 * n((N, S))).astype(np.float32),
    }

def reference(tab_words, tab_scales, offs, offs2, w1, w2_words, w2_scales, gain, w3_words, w3_scales, back):
    TW = unpack_weight(tab_words, tab_scales, "e2m1")
    v = TW[:, unstriped(offs)]
    v2 = TW[:, unstriped(offs2)]
    a = mxq(f64(w1), 0, "e4m3").T @ v
    b = unpack_weight(w2_words, w2_scales, "e4m3").T @ v2
    h = f64(gain)[:, None] * np.exp(a) / (1.0 + b * b)
    hq = mxq(h, 0, "e4m3")
    y = unpack_weight(w3_words, w3_scales, "e2m1").T @ hq
    return y + f64(back)

@@ -1,0 +1,243 @@
+from contextlib import ExitStack
+
+import concourse.mybir as mybir
+
+K, T, S, H, N = 1024, 4096, 1024, 1024, 512
+FLOPS = 2 * (2 * K * H * S + H * N * S)
+
+F32 = mybir.dt.float32
+BF16 = mybir.dt.bfloat16
+I32 = mybir.dt.int32
+U32 = mybir.dt.uint32
+U16 = mybir.dt.uint16
+U8 = mybir.dt.uint8
+FP8X4 = mybir.dt.float8_e4m3fn_x4
+FP4X4 = mybir.dt.float4_e2m1fn_x4
+ALU = mybir.AluOpType
+ACT = mybir.ActivationFunctionType
+
+P = 128
+HALF = 512
+PIECES = ((0, 256), (256, 256), (512, 256), (768, 128), (896, 128))
+TINY = 2.0 ** -64
+
+
+def tile_list_livestock_movement_scores_kernel(tc, tab_words, tab_scales, offs, offs2, w1, w2_words, w2_scales, gain, w3_words, w3_scales, back, out):
+    nc = tc.nc
+    with ExitStack() as ctx:
+        keep = ctx.enter_context(tc.tile_pool(name="keep", bufs=1))
+        ring = ctx.enter_context(tc.tile_pool(name="ring", bufs=2))
+        ps_b = ctx.enter_context(tc.psum_pool(name="ps_b", bufs=4))
+        ps_a = ctx.enter_context(tc.psum_pool(name="ps_a", bufs=2))
+        ps_y = ctx.enter_context(tc.psum_pool(name="ps_y", bufs=2))
+
+        def held(name, shape, dtype, tag="", bufs=1):
+            return keep.tile(shape, dtype, name=name, tag=tag or name, bufs=bufs, align_bytes=64)
+
+        list_a = keep.tile([P, S // 16], U16, name="list_a")
+        list_b = keep.tile([P, S // 16], U16, name="list_b")
+        tab_s = held("tab_s", [P, T], U8, "planes")
+        gain_t = held("gain_t", [P, 2, 4], F32, "words0")
+        mag = held("mag", [P, 8], F32, "table1")
+        positive = held("positive", [P, 8], F32)
+        w2_sraw = held("w2_sraw", [P, 2, H], U8, "stream")
+        mag_c = held("mag_c", [P, 8], F32)
+        sign = held("sign", [P, 2, 4], F32)
+        negated = held("negated", [P, 8], F32, "words1")
+        tab_w = [held("tab_w0", [P, T], U16, "table0")]
+        got_first = held("got_first", [P, 2, HALF], U16)
+        got_w = {(1, a, 0): got_first[:, a, :] for a in range(2)}
+        got_s = {1: held("got_sb", [P, S], U8)}
+        got_s1 = [held("got_s1%d" % l, [P, S], U8) for l in range(2)]
+        w2_c = [held("w2_c%d" % g, [P, 2, HALF], I32) for g in range(2)]
+        w2_s = [held("w2_s%d" % g, [P, 2, HALF], U8) for g in range(2)]
+        w1_c = [[held("w1_c%d%d" % (g, a), [P, HALF], U32) for a in range(2)] for g in range(2)]
+        w1_s = [[held("w1_s%d%d" % (g, a), [P, HALF], U8) for a in range(2)] for g in range(2)]
+        expo = [[held("expo%d%d" % (hf, g), [P, 4, HALF], F32) for g in range(2)] for hf in range(2)]
+
+        nc.vector.memset(tab_s[:].bitcast(I32), 0)
+        nc.vector.memset(w2_sraw[:].rearrange("p a c -> p (a c)").bitcast(I32), 0)
+        for l in (1, 0):
+            nc.gpsimd.memset(got_s1[l][:].bitcast(I32), 0)
+
+        def load_w1(g, a):
+            rows = w1[512 * a : 512 * (a + 1), HALF * g : HALF * (g + 1)]
+            nc.sync.dma_start(out=w1_raw[:, 2 * g + a], in_=rows.rearrange("(p j) c -> p j c", j=4))
+
+        def load_planes(plane, scales):
+            for q in range(4):
+                nc.sync.dma_start(out=plane[32 * q : 32 * q + 4].bitcast(I32),
+                                  in_=scales[:, 4 * q : 4 * q + 4, :].rearrange("a r c -> r a c").bitcast(I32))
+
+        nc.sync.dma_start(list_b[:], offs2)
+        nc.sync.dma_start(out=gain_t[:], in_=gain.rearrange("(g p t) -> p g t", g=2, t=4))
+        nc.sync.dma_start(list_a[:], offs)
+        nc.sync.dma_start(out=tab_w[0][:].bitcast(I32), in_=tab_words[0].bitcast(I32))
+        ts_rows = tab_scales.rearrange("a (q r) c -> r q a c", r=4)
+        for r in range(4):
+            nc.sync.dma_start(out=tab_s[r:P:16, :].bitcast(I32), in_=ts_rows[r].bitcast(I32))
+        load_planes(w2_sraw, w2_scales)
+
+        g_flat = gain_t[:].rearrange("p g t -> p (g t)")
+        log_gain = held("log_gain", [P, 8], F32)
+        sign_pat = held("sign_pat", [P, 2, P, 4], BF16)
+        nc.vector.tensor_scalar(out=negated[:], in0=g_flat, scalar1=-1.0, scalar2=None, op0=ALU.mult)
+        nc.vector.tensor_scalar(out=positive[:], in0=g_flat, scalar1=0.0, scalar2=None, op0=ALU.is_ge)
+        nc.vector.tensor_tensor(out=mag[:], in0=negated[:], in1=g_flat, op=ALU.max)
+        nc.vector.tensor_scalar(out=mag_c[:], in0=mag[:], scalar1=TINY, scalar2=None, op0=ALU.max)
+        nc.vector.tensor_scalar(out=sign[:].rearrange("p g t -> p (g t)"), in0=positive[:], scalar1=2.0, scalar2=-1.0,
+                                op0=ALU.mult, op1=ALU.add)
+        nc.scalar.activation(out=log_gain[:], in_=mag_c[:], func=ACT.Ln)
+
+        for g in range(2):
+            nc.scalar.copy(out=sign_pat[:, g], in_=sign[:, g : g + 1, :].to_broadcast([P, P, 4]))
+        tab_w.append(held("tab_w1", [P, T], U16, "table1"))
+        nc.sync.dma_start(out=tab_w[1][:].bitcast(I32), in_=tab_words[1].bitcast(I32))
+        w2_raw = [held("w2_raw%d" % g, [P, 2, HALF], I32, "words%d" % g) for g in range(2)]
+        for g in range(2):
+            words = w2_words.rearrange("a p c i -> p a (c i)")[:, :, 4 * HALF * g : 4 * HALF * (g + 1)]
+            nc.sync.dma_start(out=w2_raw[g][:], in_=words.bitcast(I32))
+
+        lists = (list_a, list_b)
+
+        def gather_scales(l):
+            nc.vector.tensor_copy(got_s[l][:], tab_s[:].indirect(lists[l][:]))
+            for r in range(4):
+                nc.sync.dma_start(out=got_s1[l][r:P:32, :].bitcast(I32), in_=got_s[l][16 + r : P : 32, :].bitcast(I32))
+
+        def gather_words(l, a, hf):
+            nc.vector.tensor_copy(got_w[l, a, hf],
+                                  tab_w[a][:].indirect(lists[l][:, 32 * hf : 32 * (hf + 1)]))
+
+        def order_w2_scales(g):
+            nc.vector.tensor_copy(out=w2_s[g][:].rearrange("p a (t m) -> p a m t", t=4),
+                                  in_=w2_sraw[:, :, HALF * g : HALF * (g + 1)].rearrange("p a (m t) -> p a m t", t=4))
+
+        def order_w2(g):
+            nc.vector.tensor_copy(out=w2_c[g][:].rearrange("p a (t m) -> p a m t", t=4),
+                                  in_=w2_raw[g][:].rearrange("p a (m t) -> p a m t", t=4))
+
+        grouped = {}
+
+        def cast_w1(g, a, on_scalar):
+            grouped[g, a] = held("grouped%d%d" % (g, a), [P, 4 * HALF], BF16, ("cast0", "cast1", "cast0", "cast2")[2 * g + a])
+            dst = grouped[g, a][:].rearrange("p (t m j) -> p m j t", t=4, j=4)
+            src = w1_raw[:, 2 * g + a].rearrange("p j (m t) -> p m j t", t=4)
+            if on_scalar:
+                nc.scalar.copy(out=dst, in_=src)
+            else:
+                nc.vector.tensor_copy(out=dst, in_=src)
+
+        def quantize_w1(g, a):
+            nc.vector.quantize_mx(out=w1_c[g][a][:].bitcast(FP8X4), scales=w1_s[g][a][:], in_=grouped[g, a][:])
+
+        def first_product(acc, l, hf, codes, scales):
+            cols = slice(HALF * hf, HALF * (hf + 1))
+            for a in range(2):
+                nc.tensor.matmul_mx(out=acc[:], lhsT=codes[a].bitcast(FP8X4), lhsT_scale=scales[a],
+                                    rhs=got_w[l, a, hf].bitcast(FP4X4),
+                                    rhs_scale=(got_s, got_s1)[a][l][:, cols], start=(a == 0), stop=(a == 1))
+
+        def damping(hf, g):
+            squares = keep.tile([P, 4 * HALF], F32, name="squares", tag="stage", align_bytes=64)
+            for t in range(4):
+                acc = ps_b.tile([P, HALF], F32, name="acc_b")
+                m = slice(P * t, P * (t + 1))
+                first_product(acc, 1, hf, [w2_c[g][:, a, m] for a in range(2)], [w2_s[g][:, a, m] for a in range(2)])
+                nc.scalar.activation(out=squares[:, HALF * t : HALF * (t + 1)], in_=acc[:], func=ACT.Square)
+            nc.scalar.activation(out=expo[hf][g][:].rearrange("p t j -> p (t j)"), in_=squares[:], func=ACT.Ln, bias=1.0)
+
+        def exponent(hf, g):
+            for t in range(4):
+                acc = ps_a.tile([P, HALF], F32, name="acc_a")
+                m = slice(P * t, P * (t + 1))
+                first_product(acc, 0, hf, [w1_c[g][a][:, m] for a in range(2)], [w1_s[g][a][:, m] for a in range(2)])
+                nc.vector.scalar_tensor_tensor(out=expo[hf][g][:, t, :], in0=acc[:],
+                                               scalar=log_gain[:, 4 * g + t : 4 * g + t + 1], in1=expo[hf][g][:, t, :],
+                                               op0=ALU.add, op1=ALU.subtract)
+
+        gather_words(1, 0, 0)
+        gather_scales(1)
+        order_w2_scales(0)
+        order_w2_scales(1)
+        w1_raw = held("w1_raw", [P, 4, 4, HALF], F32, "stream")
+        for g in range(2):
+            for a in range(2):
+                load_w1(g, a)
+        gather_words(1, 1, 0)
+        order_w2(0)
+        damping(0, 0)
+        cast_w1(0, 0, True)
+        order_w2(1)
+        got_s[0] = held("got_sa", [P, S], U8, "words0")
+        got_rest = held("got_rest", [P, 4, HALF], U16, "words1")
+        for i, key in enumerate(((1, 0, 1), (1, 1, 1), (0, 0, 0), (0, 1, 0))):
+            got_w[key] = got_rest[:, i, :]
+        gather_words(1, 0, 1)
+        gather_words(1, 1, 1)
+        gather_scales(0)
+        w3_all = held("w3_all", [P, 6 * N], U8, "planes")
+        w3_w = w3_all[:, : 4 * N].rearrange("p (a c) -> p a c", a=2)
+        w3_s = w3_all[:, 4 * N :].rearrange("p (a c) -> p a c", a=2)
+        nc.gpsimd.memset(w3_all[:, 4 * N :].bitcast(I32), 0)
+        gather_words(0, 0, 0)
+        gather_words(0, 1, 0)
+        cast_w1(0, 1, False)
+        damping(0, 1)
+        quantize_w1(0, 0)
+        quantize_w1(0, 1)
+        cast_w1(1, 0, True)
+        exponent(0, 0)
+        damping(1, 0)
+        got_last = held("got_last", [P, 2, HALF], U16, "cast1")
+        for a in range(2):
+            got_w[0, a, 1] = got_last[:, a, :]
+            gather_words(0, a, 1)
+        cast_w1(1, 1, False)
+        quantize_w1(1, 0)
+        quantize_w1(1, 1)
+        damping(1, 1)
+        load_planes(w3_s, w3_scales)
+        nc.sync.dma_start(out=w3_w.bitcast(I32), in_=w3_words.rearrange("a p c -> p a c").bitcast(I32))
+        back_t = [held("back%d" % hf, [P, 4, HALF], F32, "table%d" % hf) for hf in range(2)]
+        for hf in range(2):
+            nc.sync.dma_start(out=back_t[hf][:],
+                              in_=back[:, HALF * hf : HALF * (hf + 1)].rearrange("(n p) j -> p n j", p=P))
+        exponent(0, 1)
+        exponent(1, 0)
+        exponent(1, 1)
+
+        h_abs = keep.tile([P, 8 * S], BF16, name="h_abs", tag="stage", align_bytes=64)
+        h_c = held("h_c", [P, 2 * S], U32)
+        h_s = held("h_s", [P, 2 * S], U8)
+        out_rows = out.rearrange("(n p) j -> p n j", p=P)
+        for j0, width in PIECES:
+            hf, lo = divmod(j0, HALF)
+            for g in range(2):
+                c0 = 4 * (2 * j0 + g * width)
+                nc.scalar.activation(
+                    out=h_abs[:, c0 : c0 + 4 * width].rearrange("p (c i t) -> p c t i", i=4, t=4),
+                    in_=expo[hf][g][:, :, lo : lo + width].rearrange("p t (c i) -> p c t i", i=4), func=ACT.Exp)
+            h = ring.tile([P, 8 * width], BF16, name="h", align_bytes=64)
+            reps = width // P
+            nc.vector.tensor_tensor(
+                out=h[:].rearrange("p (g u e) -> p g u e", g=2, u=reps),
+                in0=h_abs[:, 8 * j0 : 8 * (j0 + width)].rearrange("p (g u e) -> p g u e", g=2, u=reps),
+                in1=sign_pat[:].rearrange("p g j t -> p g (j t)").unsqueeze(2).to_broadcast([P, 2, reps, 4 * P]),
+                op=ALU.mult)
+            nc.vector.quantize_mx(out=h_c[:, 2 * j0 : 2 * (j0 + width)].bitcast(FP8X4),
+                                  scales=h_s[:, 2 * j0 : 2 * (j0 + width)], in_=h[:])
+            res = held("res%d" % j0, [P, 4, width], F32)
+            for u in range(reps):
+                acc = ps_y.tile([P, 4, P], F32, name="acc_y")
+                for n in range(4):
+                    for g in range(2):
+                        c0 = 2 * j0 + g * width + P * u
+                        nc.tensor.matmul_mx(out=acc[:, n, :],
+                                            lhsT=w3_w[:, g, 2 * P * n : 2 * P * (n + 1)].bitcast(FP4X4),
+                                            lhsT_scale=w3_s[:, g, P * n : P * (n + 1)],
+                                            rhs=h_c[:, c0 : c0 + P].bitcast(FP8X4), rhs_scale=h_s[:, c0 : c0 + P],
+                                            start=(g == 0), stop=(g == 1))
+                nc.vector.tensor_tensor(out=res[:, :, P * u : P * (u + 1)], in0=acc[:],
+                                        in1=back_t[hf][:, :, lo + P * u : lo + P * (u + 1)], op=ALU.add)
+            nc.sync.dma_start(out=out_rows[:, :, j0 : j0 + width], in_=res[:])

@@ -18,7 +18,7 @@ ACT = mybir.ActivationFunctionType
 
 P = 128
 HALF = 512
-PIECES = ((0, 256), (256, 256), (512, 256), (768, 128), (896, 128))
+PIECES = ((0, 128), (128, 128), (256, 256), (512, 256), (768, 128), (896, 128))
 TINY = 2.0 ** -64
 
 
@@ -28,8 +28,7 @@ def tile_list_livestock_movement_scores_kernel(tc, tab_words, tab_scales, offs, 
         keep = ctx.enter_context(tc.tile_pool(name="keep", bufs=1))
         ring = ctx.enter_context(tc.tile_pool(name="ring", bufs=2))
         ps_b = ctx.enter_context(tc.psum_pool(name="ps_b", bufs=4))
-        ps_a = ctx.enter_context(tc.psum_pool(name="ps_a", bufs=2))
-        ps_y = ctx.enter_context(tc.psum_pool(name="ps_y", bufs=2))
+        ps_a = ctx.enter_context(tc.psum_pool(name="ps_a", bufs=4))
 
         def held(name, shape, dtype, tag="", bufs=1):
             return keep.tile(shape, dtype, name=name, tag=tag or name, bufs=bufs, align_bytes=64)
@@ -120,10 +119,14 @@ def tile_list_livestock_movement_scores_kernel(tc, tab_words, tab_scales, offs, 
         grouped = {}
 
         def cast_w1(g, a, on_scalar):
-            grouped[g, a] = held("grouped%d%d" % (g, a), [P, 4 * HALF], BF16, ("cast0", "cast1", "cast0", "cast2")[2 * g + a])
+            grouped[g, a] = held("grouped%d%d" % (g, a), [P, 4 * HALF], BF16, "cast%d" % (2 * g + a))
             dst = grouped[g, a][:].rearrange("p (t m j) -> p m j t", t=4, j=4)
             src = w1_raw[:, 2 * g + a].rearrange("p j (m t) -> p m j t", t=4)
-            if on_scalar:
+            if g == 1:
+                for m0 in range(0, P, 32):
+                    nc.gpsimd.tensor_scalar(out=dst[:, m0 : m0 + 32], in0=src[:, m0 : m0 + 32], scalar1=1.0, scalar2=0.0,
+                                            op0=ALU.mult, op1=ALU.add)
+            elif on_scalar:
                 nc.scalar.copy(out=dst, in_=src)
             else:
                 nc.vector.tensor_copy(out=dst, in_=src)
@@ -229,7 +232,7 @@ def tile_list_livestock_movement_scores_kernel(tc, tab_words, tab_scales, offs, 
                                   scales=h_s[:, 2 * j0 : 2 * (j0 + width)], in_=h[:])
             res = held("res%d" % j0, [P, 4, width], F32)
             for u in range(reps):
-                acc = ps_y.tile([P, 4, P], F32, name="acc_y")
+                acc = ps_b.tile([P, 4, P], F32, name="acc_y", tag="acc_b")
                 for n in range(4):
                     for g in range(2):
                         c0 = 2 * j0 + g * width + P * u

@@ -118,18 +118,13 @@ def tile_list_livestock_movement_scores_kernel(tc, tab_words, tab_scales, offs, 
 
         grouped = {}
 
-        def cast_w1(g, a, on_scalar):
+        def cast_w1(g, a):
             grouped[g, a] = held("grouped%d%d" % (g, a), [P, 4 * HALF], BF16, "cast%d" % (2 * g + a))
             dst = grouped[g, a][:].rearrange("p (t m j) -> p m j t", t=4, j=4)
             src = w1_raw[:, 2 * g + a].rearrange("p j (m t) -> p m j t", t=4)
-            if g == 1:
-                for m0 in range(0, P, 32):
-                    nc.gpsimd.tensor_scalar(out=dst[:, m0 : m0 + 32], in0=src[:, m0 : m0 + 32], scalar1=1.0, scalar2=0.0,
-                                            op0=ALU.mult, op1=ALU.add)
-            elif on_scalar:
-                nc.scalar.copy(out=dst, in_=src)
-            else:
-                nc.vector.tensor_copy(out=dst, in_=src)
+            for m0 in range(0, P, 32):
+                nc.gpsimd.tensor_scalar(out=dst[:, m0 : m0 + 32], in0=src[:, m0 : m0 + 32], scalar1=1.0, scalar2=0.0,
+                                        op0=ALU.mult, op1=ALU.add)
 
         def quantize_w1(g, a):
             nc.vector.quantize_mx(out=w1_c[g][a][:].bitcast(FP8X4), scales=w1_s[g][a][:], in_=grouped[g, a][:])
@@ -170,7 +165,7 @@ def tile_list_livestock_movement_scores_kernel(tc, tab_words, tab_scales, offs, 
         gather_words(1, 1, 0)
         order_w2(0)
         damping(0, 0)
-        cast_w1(0, 0, True)
+        cast_w1(0, 0)
         order_w2(1)
         got_s[0] = held("got_sa", [P, S], U8, "words0")
         got_rest = held("got_rest", [P, 4, HALF], U16, "words1")
@@ -185,18 +180,18 @@ def tile_list_livestock_movement_scores_kernel(tc, tab_words, tab_scales, offs, 
         nc.gpsimd.memset(w3_all[:, 4 * N :].bitcast(I32), 0)
         gather_words(0, 0, 0)
         gather_words(0, 1, 0)
-        cast_w1(0, 1, False)
+        cast_w1(0, 1)
         damping(0, 1)
         quantize_w1(0, 0)
         quantize_w1(0, 1)
-        cast_w1(1, 0, True)
+        cast_w1(1, 0)
         exponent(0, 0)
         damping(1, 0)
         got_last = held("got_last", [P, 2, HALF], U16, "cast1")
         for a in range(2):
             got_w[0, a, 1] = got_last[:, a, :]
             gather_words(0, a, 1)
-        cast_w1(1, 1, False)
+        cast_w1(1, 1)
         quantize_w1(1, 0)
         quantize_w1(1, 1)
         damping(1, 1)

from contextlib import ExitStack

import concourse.mybir as mybir

K, T, S, H, N = 1024, 4096, 1024, 1024, 512
FLOPS = 2 * (2 * K * H * S + H * N * S)

F32 = mybir.dt.float32
BF16 = mybir.dt.bfloat16
I32 = mybir.dt.int32
U32 = mybir.dt.uint32
U16 = mybir.dt.uint16
U8 = mybir.dt.uint8
FP8X4 = mybir.dt.float8_e4m3fn_x4
FP4X4 = mybir.dt.float4_e2m1fn_x4
ALU = mybir.AluOpType
ACT = mybir.ActivationFunctionType

P = 128
HALF = 512
PIECES = ((0, 128), (128, 128), (256, 256), (512, 256), (768, 128), (896, 128))
TINY = 2.0 ** -64


def tile_list_livestock_movement_scores_kernel(tc, tab_words, tab_scales, offs, offs2, w1, w2_words, w2_scales, gain, w3_words, w3_scales, back, out):
    nc = tc.nc
    with ExitStack() as ctx:
        keep = ctx.enter_context(tc.tile_pool(name="keep", bufs=1))
        ring = ctx.enter_context(tc.tile_pool(name="ring", bufs=2))
        ps_b = ctx.enter_context(tc.psum_pool(name="ps_b", bufs=4))
        ps_a = ctx.enter_context(tc.psum_pool(name="ps_a", bufs=4))

        def held(name, shape, dtype, tag="", bufs=1):
            return keep.tile(shape, dtype, name=name, tag=tag or name, bufs=bufs, align_bytes=64)

        list_a = keep.tile([P, S // 16], U16, name="list_a")
        list_b = keep.tile([P, S // 16], U16, name="list_b")
        tab_s = held("tab_s", [P, T], U8, "planes")
        gain_t = held("gain_t", [P, 2, 4], F32, "words0")
        mag = held("mag", [P, 8], F32, "table1")
        positive = held("positive", [P, 8], F32)
        w2_sraw = held("w2_sraw", [P, 2, H], U8, "stream")
        mag_c = held("mag_c", [P, 8], F32)
        sign = held("sign", [P, 2, 4], F32)
        negated = held("negated", [P, 8], F32, "words1")
        tab_w = [held("tab_w0", [P, T], U16, "table0")]
        got_first = held("got_first", [P, 2, HALF], U16)
        got_w = {(1, a, 0): got_first[:, a, :] for a in range(2)}
        got_s = {1: held("got_sb", [P, S], U8)}
        got_s1 = [held("got_s1%d" % l, [P, S], U8) for l in range(2)]
        w2_c = [held("w2_c%d" % g, [P, 2, HALF], I32) for g in range(2)]
        w2_s = [held("w2_s%d" % g, [P, 2, HALF], U8) for g in range(2)]
        w1_c = [[held("w1_c%d%d" % (g, a), [P, HALF], U32) for a in range(2)] for g in range(2)]
        w1_s = [[held("w1_s%d%d" % (g, a), [P, HALF], U8) for a in range(2)] for g in range(2)]
        expo = [[held("expo%d%d" % (hf, g), [P, 4, HALF], F32) for g in range(2)] for hf in range(2)]

        nc.vector.memset(tab_s[:].bitcast(I32), 0)
        nc.vector.memset(w2_sraw[:].rearrange("p a c -> p (a c)").bitcast(I32), 0)
        for l in (1, 0):
            nc.gpsimd.memset(got_s1[l][:].bitcast(I32), 0)

        def load_w1(g, a):
            rows = w1[512 * a : 512 * (a + 1), HALF * g : HALF * (g + 1)]
            nc.sync.dma_start(out=w1_raw[:, 2 * g + a], in_=rows.rearrange("(p j) c -> p j c", j=4))

        def load_planes(plane, scales):
            for q in range(4):
                nc.sync.dma_start(out=plane[32 * q : 32 * q + 4].bitcast(I32),
                                  in_=scales[:, 4 * q : 4 * q + 4, :].rearrange("a r c -> r a c").bitcast(I32))

        nc.sync.dma_start(list_b[:], offs2)
        nc.sync.dma_start(out=gain_t[:], in_=gain.rearrange("(g p t) -> p g t", g=2, t=4))
        nc.sync.dma_start(list_a[:], offs)
        nc.sync.dma_start(out=tab_w[0][:].bitcast(I32), in_=tab_words[0].bitcast(I32))
        ts_rows = tab_scales.rearrange("a (q r) c -> r q a c", r=4)
        for r in range(4):
            nc.sync.dma_start(out=tab_s[r:P:16, :].bitcast(I32), in_=ts_rows[r].bitcast(I32))
        load_planes(w2_sraw, w2_scales)

        g_flat = gain_t[:].rearrange("p g t -> p (g t)")
        log_gain = held("log_gain", [P, 8], F32)
        sign_pat = held("sign_pat", [P, 2, P, 4], BF16)
        nc.vector.tensor_scalar(out=negated[:], in0=g_flat, scalar1=-1.0, scalar2=None, op0=ALU.mult)
        nc.vector.tensor_scalar(out=positive[:], in0=g_flat, scalar1=0.0, scalar2=None, op0=ALU.is_ge)
        nc.vector.tensor_tensor(out=mag[:], in0=negated[:], in1=g_flat, op=ALU.max)
        nc.vector.tensor_scalar(out=mag_c[:], in0=mag[:], scalar1=TINY, scalar2=None, op0=ALU.max)
        nc.vector.tensor_scalar(out=sign[:].rearrange("p g t -> p (g t)"), in0=positive[:], scalar1=2.0, scalar2=-1.0,
                                op0=ALU.mult, op1=ALU.add)
        nc.scalar.activation(out=log_gain[:], in_=mag_c[:], func=ACT.Ln)

        for g in range(2):
            nc.scalar.copy(out=sign_pat[:, g], in_=sign[:, g : g + 1, :].to_broadcast([P, P, 4]))
        tab_w.append(held("tab_w1", [P, T], U16, "table1"))
        nc.sync.dma_start(out=tab_w[1][:].bitcast(I32), in_=tab_words[1].bitcast(I32))
        w2_raw = [held("w2_raw%d" % g, [P, 2, HALF], I32, "words%d" % g) for g in range(2)]
        for g in range(2):
            words = w2_words.rearrange("a p c i -> p a (c i)")[:, :, 4 * HALF * g : 4 * HALF * (g + 1)]
            nc.sync.dma_start(out=w2_raw[g][:], in_=words.bitcast(I32))

        lists = (list_a, list_b)

        def gather_scales(l):
            nc.vector.tensor_copy(got_s[l][:], tab_s[:].indirect(lists[l][:]))
            for r in range(4):
                nc.sync.dma_start(out=got_s1[l][r:P:32, :].bitcast(I32), in_=got_s[l][16 + r : P : 32, :].bitcast(I32))

        def gather_words(l, a, hf):
            nc.vector.tensor_copy(got_w[l, a, hf],
                                  tab_w[a][:].indirect(lists[l][:, 32 * hf : 32 * (hf + 1)]))

        def order_w2_scales(g):
            nc.vector.tensor_copy(out=w2_s[g][:].rearrange("p a (t m) -> p a m t", t=4),
                                  in_=w2_sraw[:, :, HALF * g : HALF * (g + 1)].rearrange("p a (m t) -> p a m t", t=4))

        def order_w2(g):
            nc.vector.tensor_copy(out=w2_c[g][:].rearrange("p a (t m) -> p a m t", t=4),
                                  in_=w2_raw[g][:].rearrange("p a (m t) -> p a m t", t=4))

        grouped = {}

        def cast_w1(g, a):
            grouped[g, a] = held("grouped%d%d" % (g, a), [P, 4 * HALF], BF16, "cast%d" % (2 * g + a))
            dst = grouped[g, a][:].rearrange("p (t m j) -> p m j t", t=4, j=4)
            src = w1_raw[:, 2 * g + a].rearrange("p j (m t) -> p m j t", t=4)
            for m0 in range(0, P, 32):
                nc.gpsimd.tensor_scalar(out=dst[:, m0 : m0 + 32], in0=src[:, m0 : m0 + 32], scalar1=1.0, scalar2=0.0,
                                        op0=ALU.mult, op1=ALU.add)

        def quantize_w1(g, a):
            nc.vector.quantize_mx(out=w1_c[g][a][:].bitcast(FP8X4), scales=w1_s[g][a][:], in_=grouped[g, a][:])

        def first_product(acc, l, hf, codes, scales):
            cols = slice(HALF * hf, HALF * (hf + 1))
            for a in range(2):
                nc.tensor.matmul_mx(out=acc[:], lhsT=codes[a].bitcast(FP8X4), lhsT_scale=scales[a],
                                    rhs=got_w[l, a, hf].bitcast(FP4X4),
                                    rhs_scale=(got_s, got_s1)[a][l][:, cols], start=(a == 0), stop=(a == 1))

        def damping(hf, g):
            squares = keep.tile([P, 4 * HALF], F32, name="squares", tag="stage", align_bytes=64)
            for t in range(4):
                acc = ps_b.tile([P, HALF], F32, name="acc_b")
                m = slice(P * t, P * (t + 1))
                first_product(acc, 1, hf, [w2_c[g][:, a, m] for a in range(2)], [w2_s[g][:, a, m] for a in range(2)])
                nc.scalar.activation(out=squares[:, HALF * t : HALF * (t + 1)], in_=acc[:], func=ACT.Square)
            nc.scalar.activation(out=expo[hf][g][:].rearrange("p t j -> p (t j)"), in_=squares[:], func=ACT.Ln, bias=1.0)

        def exponent(hf, g):
            for t in range(4):
                acc = ps_a.tile([P, HALF], F32, name="acc_a")
                m = slice(P * t, P * (t + 1))
                first_product(acc, 0, hf, [w1_c[g][a][:, m] for a in range(2)], [w1_s[g][a][:, m] for a in range(2)])
                nc.vector.scalar_tensor_tensor(out=expo[hf][g][:, t, :], in0=acc[:],
                                               scalar=log_gain[:, 4 * g + t : 4 * g + t + 1], in1=expo[hf][g][:, t, :],
                                               op0=ALU.add, op1=ALU.subtract)

        gather_words(1, 0, 0)
        gather_scales(1)
        order_w2_scales(0)
        order_w2_scales(1)
        w1_raw = held("w1_raw", [P, 4, 4, HALF], F32, "stream")
        for g in range(2):
            for a in range(2):
                load_w1(g, a)
        gather_words(1, 1, 0)
        order_w2(0)
        damping(0, 0)
        cast_w1(0, 0)
        order_w2(1)
        got_s[0] = held("got_sa", [P, S], U8, "words0")
        got_rest = held("got_rest", [P, 4, HALF], U16, "words1")
        for i, key in enumerate(((1, 0, 1), (1, 1, 1), (0, 0, 0), (0, 1, 0))):
            got_w[key] = got_rest[:, i, :]
        gather_words(1, 0, 1)
        gather_words(1, 1, 1)
        gather_scales(0)
        w3_all = held("w3_all", [P, 6 * N], U8, "planes")
        w3_w = w3_all[:, : 4 * N].rearrange("p (a c) -> p a c", a=2)
        w3_s = w3_all[:, 4 * N :].rearrange("p (a c) -> p a c", a=2)
        nc.gpsimd.memset(w3_all[:, 4 * N :].bitcast(I32), 0)
        gather_words(0, 0, 0)
        gather_words(0, 1, 0)
        cast_w1(0, 1)
        damping(0, 1)
        quantize_w1(0, 0)
        quantize_w1(0, 1)
        cast_w1(1, 0)
        exponent(0, 0)
        damping(1, 0)
        got_last = held("got_last", [P, 2, HALF], U16, "cast1")
        for a in range(2):
            got_w[0, a, 1] = got_last[:, a, :]
            gather_words(0, a, 1)
        cast_w1(1, 1)
        quantize_w1(1, 0)
        quantize_w1(1, 1)
        damping(1, 1)
        load_planes(w3_s, w3_scales)
        nc.sync.dma_start(out=w3_w.bitcast(I32), in_=w3_words.rearrange("a p c -> p a c").bitcast(I32))
        back_t = [held("back%d" % hf, [P, 4, HALF], F32, "table%d" % hf) for hf in range(2)]
        for hf in range(2):
            nc.sync.dma_start(out=back_t[hf][:],
                              in_=back[:, HALF * hf : HALF * (hf + 1)].rearrange("(n p) j -> p n j", p=P))
        exponent(0, 1)
        exponent(1, 0)
        exponent(1, 1)

        h_abs = keep.tile([P, 8 * S], BF16, name="h_abs", tag="stage", align_bytes=64)
        h_c = held("h_c", [P, 2 * S], U32)
        h_s = held("h_s", [P, 2 * S], U8)
        out_rows = out.rearrange("(n p) j -> p n j", p=P)
        for j0, width in PIECES:
            hf, lo = divmod(j0, HALF)
            for g in range(2):
                c0 = 4 * (2 * j0 + g * width)
                nc.scalar.activation(
                    out=h_abs[:, c0 : c0 + 4 * width].rearrange("p (c i t) -> p c t i", i=4, t=4),
                    in_=expo[hf][g][:, :, lo : lo + width].rearrange("p t (c i) -> p c t i", i=4), func=ACT.Exp)
            h = ring.tile([P, 8 * width], BF16, name="h", align_bytes=64)
            reps = width // P
            nc.vector.tensor_tensor(
                out=h[:].rearrange("p (g u e) -> p g u e", g=2, u=reps),
                in0=h_abs[:, 8 * j0 : 8 * (j0 + width)].rearrange("p (g u e) -> p g u e", g=2, u=reps),
                in1=sign_pat[:].rearrange("p g j t -> p g (j t)").unsqueeze(2).to_broadcast([P, 2, reps, 4 * P]),
                op=ALU.mult)
            nc.vector.quantize_mx(out=h_c[:, 2 * j0 : 2 * (j0 + width)].bitcast(FP8X4),
                                  scales=h_s[:, 2 * j0 : 2 * (j0 + width)], in_=h[:])
            res = held("res%d" % j0, [P, 4, width], F32)
            for u in range(reps):
                acc = ps_b.tile([P, 4, P], F32, name="acc_y", tag="acc_b")
                for n in range(4):
                    for g in range(2):
                        c0 = 2 * j0 + g * width + P * u
                        nc.tensor.matmul_mx(out=acc[:, n, :],
                                            lhsT=w3_w[:, g, 2 * P * n : 2 * P * (n + 1)].bitcast(FP4X4),
                                            lhsT_scale=w3_s[:, g, P * n : P * (n + 1)],
                                            rhs=h_c[:, c0 : c0 + P].bitcast(FP8X4), rhs_scale=h_s[:, c0 : c0 + P],
                                            start=(g == 0), stop=(g == 1))
                nc.vector.tensor_tensor(out=res[:, :, P * u : P * (u + 1)], in0=acc[:],
                                        in1=back_t[hf][:, :, lo + P * u : lo + P * (u + 1)], op=ALU.add)
            nc.sync.dma_start(out=out_rows[:, :, j0 : j0 + width], in_=res[:])
